import numpy as np
import ml_dtypes


def mxq(x, axis, fmt="e4m3"):
    dtype, down = {"e4m3": (ml_dtypes.float8_e4m3fn, 7), "e5m2": (ml_dtypes.float8_e5m2, 14)}[fmt]
    v = np.moveaxis(np.asarray(x, np.float32).astype(ml_dtypes.bfloat16).astype(np.float64), axis, -1)
    blocks = v.reshape(v.shape[:-1] + (-1, 32))
    amax = np.abs(blocks).max(-1, keepdims=True)
    byte = np.maximum(np.where(amax > 0, np.frexp(amax)[1] - 1 + 127, 0) - down, 1)
    scale = np.exp2(byte - 127.0)
    codes = (blocks / scale).astype(np.float32).astype(dtype).astype(np.float64)
    return np.moveaxis((codes * scale).reshape(v.shape), -1, axis)


WIDE = False


def mx_kscale(k):
    if not WIDE:
        return np.ones(k)
    levels = np.array([18, -18])
    if k % 512:
        return np.exp2(np.random.permutation(np.resize(levels, k // 32))).repeat(32)
    a = np.empty((k // 512, 16))
    for p in range(k // 512):
        a[p, :8] = np.random.permutation(np.resize(levels, 8))
        for g in range(8):
            far = levels[np.abs(levels - a[p, g]) >= 10]
            a[p, g + 8] = far[np.random.randint(len(far))]
    return np.exp2(a.ravel()).repeat(32)


def f64(x):
    return np.asarray(x).astype(np.float64)


def striped(idx):
    return np.tile(np.asarray(idx).reshape(-1, 16).T, (8, 1)).astype(np.uint16)


def unstriped(offs):
    return offs[:16].T.reshape(-1).astype(np.int64)

def planes(y):
    n, m = y.shape
    v = y.astype(np.float32).astype(ml_dtypes.bfloat16).astype(np.float64).reshape(n // 32, 32, m)
    top = np.abs(v).max(1)
    byte = np.clip(np.where(top > 0, np.frexp(top)[1] - 1 + 127 - 7, 1), 1, 254)
    codes = (v * np.exp2(127.0 - byte)[:, None, :]).reshape(n, m).astype(np.float32).astype(ml_dtypes.float8_e4m3fn).view(np.uint8)
    words = codes.reshape(n // 512, 128, 4, m).transpose(0, 1, 3, 2)
    return np.ascontiguousarray(words), np.ascontiguousarray(byte.astype(np.uint8).reshape(n // 512, 16, m))


def setup_inputs():
    n = np.random.standard_normal
    uni = np.random.uniform
    idx = np.random.permutation(2048)[:512]
    soft = np.exp(0.4 * n((512, 512)))
    soft2 = np.exp(0.4 * n((512, 512)))
    f_d = mx_kscale(512)
    f_h = mx_kscale(512)
    f_i = np.ones(2048)
    f_i[idx] = mx_kscale(512)
    return {
        "xT": (0.5 * n((512, 512)) * f_d[:, None]).astype(np.float32),
        "wT": (n((512, 2048)) / np.sqrt(512) / f_d[:, None] * f_i[None, :]).astype(np.float32),
        "hT": (n((512, 512)) / np.sqrt(512) / f_d[:, None] * f_h[None, :]).astype(np.float32),
        "us": (uni(0.75, 1.3, (512, 1))).astype(np.float32),
        "ts": np.tile(uni(0.75, 1.3, 2048) / f_i, (128, 1)).astype(np.float32),
        "th": np.tile(uni(0.75, 1.3, 512) / f_h, (128, 1)).astype(np.float32),
        "wt": (uni(0.75, 1.3, (512, 1))).astype(np.float32),
        "wh": (uni(0.75, 1.3, (512, 1))).astype(np.float32),
        "yt": (soft / soft.sum(-1, keepdims=True)).astype(np.float32),
        "yh": (soft2 / soft2.sum(-1, keepdims=True)).astype(np.float32),
        "offs": striped(idx),
    }


def reference(xT, wT, hT, us, ts, th, wt, wh, yt, yh, offs):
    idx = unstriped(offs)
    wT_i = f64(wT)[:, idx]
    ts_i = f64(ts)[:1][:, idx]
    q_xT = mxq(f64(xT), 0, "e4m3")
    a = q_xT.T @ mxq(wT_i, 0, "e4m3")
    z = f64(us) * ts_i * a
    m = (z).max(-1, keepdims=True)
    e = np.exp(z - m)
    tot = (e).sum(-1, keepdims=True)
    g = f64(wt) * f64(us) * ts_i * (e / tot - f64(yt))
    b = q_xT.T @ mxq(f64(hT), 0, "e4m3")
    zh = f64(us) * f64(th)[:1] * b
    mh = (zh).max(-1, keepdims=True)
    eh = np.exp(zh - mh)
    toth = (eh).sum(-1, keepdims=True)
    gh = f64(wh) * f64(us) * f64(th)[:1] * (eh / toth - f64(yh))
    x1 = mxq(gh, 1, "e5m2") @ mxq(f64(hT), 1, "e4m3").T
    x2 = mxq(g, 1, "e5m2") @ mxq(wT_i, 1, "e4m3").T
    out_0 = x1 + x2
    return (out_0,) + planes(out_0)

@@ -1,0 +1,279 @@
+from contextlib import ExitStack
+
+import concourse.mybir as mybir
+from concourse.masks import make_identity
+
+F32 = mybir.dt.float32
+BF16 = mybir.dt.bfloat16
+U32 = mybir.dt.uint32
+I32 = mybir.dt.int32
+U16 = mybir.dt.uint16
+U8 = mybir.dt.uint8
+E4 = mybir.dt.float8_e4m3fn_x4
+E5 = mybir.dt.float8_e5m2_x4
+ALU = mybir.AluOpType
+ACT = mybir.ActivationFunctionType
+
+P = 128
+L = 4
+N = 512
+T = 2048
+FLOPS = 4 * 2 * N * N * N
+
+
+def tile_attend_gadsm_x_pl_kernel(tc, xT, wT, hT, us, ts, th, wt, wh, yt, yh, offs, out_0, out_1, out_2):
+    nc = tc.nc
+    with ExitStack() as ctx:
+        keep = ctx.enter_context(tc.tile_pool(name="keep", bufs=1))
+        work = ctx.enter_context(tc.tile_pool(name="work", bufs=3))
+        psum = ctx.enter_context(tc.psum_pool(name="psum", bufs=2))
+
+        def kept(name, shape, dtype, tag=None):
+            return keep.tile(shape, dtype, name=name, tag=tag or name, align_bytes=64)
+
+        def block(j, width=P):
+            return slice(j * width, (j + 1) * width)
+
+        ident = kept("ident", [P, P], F32)
+        make_identity(nc, ident[:])
+        warm = kept("warm", [P, 1], F32)
+        nc.vector.memset(warm[:], 0.0)
+        nc.scalar.activation(warm[:], warm[:], ACT.Exp)
+        h_raw = kept("h_raw", [P, L * N], F32)
+        nc.sync.dma_start(out=h_raw[:], in_=hT.rearrange("(p t) r -> p (t r)", t=L))
+        x_raw = kept("x_raw", [P, L * N], F32)
+        nc.sync.dma_start(out=x_raw[:], in_=xT.rearrange("(p t) r -> p (t r)", t=L))
+
+        offsets = kept("offsets", [P, N // 16], U16)
+        nc.sync.dma_start(offsets[:], offs)
+        ts_win = kept("ts_win", [P, T], F32)
+        nc.vector.memset(ts_win[:], 0.0)
+        th_col = kept("th_col", [P, L], F32)
+        with nc.allow_non_contiguous_dma(reason="one scale a partition"):
+            nc.sync.dma_start(out=th_col[:], in_=th[0:1, :].rearrange("o (j p) -> p (o j)", j=L))
+        cols = {}
+        for name, src in (("us", us), ("wh", wh), ("wt", wt)):
+            cols[name] = kept(name + "_col", [P, L], F32)
+            nc.sync.dma_start(out=cols[name][:], in_=src.rearrange("(p j) o -> p (j o)", j=L))
+
+        nc.scalar.dma_start(out=ts_win[0:1, :], in_=ts[0:1, :])
+
+        def load_targets(name, y):
+            halves = []
+            for a in range(2):
+                half = kept(name + "%d" % a, [P, 2 * N], F32)
+                nc.sync.dma_start(out=half[:], in_=y.rearrange("(p a j) i -> a p (j i)", a=2, j=2)[a])
+                halves.append(half)
+            return [halves[j // 2][:, block(j % 2, N)] for j in range(L)]
+
+        w_raw = []
+        for t in range(L):
+            w_raw.append(kept("w_raw%d" % t, [P, T], F32))
+            nc.sync.dma_start(out=w_raw[t][:], in_=wT.rearrange("(p t) c -> t p c", t=L)[t])
+        yh_rows = load_targets("yh", yh)
+        yt_rows = load_targets("yt", yt)
+
+
+        def quantize(name, src, fmt):
+            width = src.shape[1] // L
+            codes = kept(name + "_codes", [P, width], U32)
+            scales = kept(name + "_scales", [P, width], U8)
+            nc.vector.quantize_mx(out=codes[:].bitcast(fmt), scales=scales[:], in_=src)
+            return codes, scales
+
+        def mm(out, lhs, lhs_fmt, lhs_cols, rhs, start, stop):
+            nc.tensor.matmul_mx(
+                out=out,
+                lhsT=lhs[0][:, lhs_cols].bitcast(lhs_fmt),
+                lhsT_scale=lhs[1][:, lhs_cols],
+                rhs=rhs[0][:].bitcast(E4),
+                rhs_scale=rhs[1][:],
+                start=start,
+                stop=stop,
+            )
+
+        def new_bank(tag):
+            return psum.tile([P, N], F32, name=tag, tag=tag)
+
+        h_bf = kept("h_bf", [P, L * N], BF16)
+        nc.vector.tensor_copy(
+            out=h_bf[:].rearrange("p (c i t) -> p c t i", i=L, t=L),
+            in_=h_raw[:].rearrange("p (t c i) -> p c t i", t=L, i=L),
+        )
+        hq = quantize("h", h_bf[:], E4)
+
+        S = 3 * N
+        arena = kept("arena", [P, L * S], BF16)
+        x_bf = arena[:, 0 : L * N]
+        nc.vector.tensor_copy(
+            out=x_bf.rearrange("p (j q t) -> p q t j", j=L, t=L),
+            in_=x_raw[:].rearrange("p (t q j) -> p q t j", t=L, j=L),
+        )
+        xq = quantize("x", x_bf, E4)
+
+        h_words = h_bf[:].bitcast(F32)
+        h_turned = kept("h_turned", [P, L * N], BF16)
+        for v in range(2):
+            bank = new_bank("score" if v == 0 else "zbank")
+            for t in range(L):
+                nc.tensor.transpose(bank[:, block(t)], h_words[:, 2 * t + v : 2 * N : 8], ident[:])
+            nc.scalar.copy(
+                out=h_turned[:].rearrange("q (p v e t) -> q v p e t", v=2, e=2, t=L)[:, v],
+                in_=bank[:].bitcast(BF16).rearrange("q (t p e) -> q p e t", t=L, e=2),
+            )
+
+        neg_us = kept("neg_us", [P, L], F32)
+        nc.gpsimd.tensor_scalar(neg_us[:], cols["us"][:], -1.0, 0.0, ALU.mult, ALU.add)
+        c_head = kept("c_head", [P, L], F32)
+        nc.gpsimd.tensor_tensor(c_head[:], cols["wh"][:], cols["us"][:], ALU.mult)
+        c_tail = kept("c_tail", [P, L], F32)
+        nc.gpsimd.tensor_tensor(c_tail[:], cols["wt"][:], cols["us"][:], ALU.mult)
+
+        def spread(name, col):
+            bank = new_bank("zbank")
+            for j in range(L):
+                nc.tensor.transpose(bank[:, block(j)], col[:, j : j + 1].to_broadcast([P, P]), ident[:])
+            rows = kept(name, [P, N], F32)
+            nc.scalar.copy(out=rows[:], in_=bank[:])
+            return rows
+
+        def scores(name, b, lhs, lhs_cols, col):
+            bank = new_bank("score")
+            mm(bank[:], lhs, E4, lhs_cols, xq, True, True)
+            scaled = kept(name + "%d" % b, [P, N], F32)
+            nc.scalar.activation(scaled[:], bank[:], ACT.Copy, scale=col[:, b : b + 1])
+            return scaled
+
+        def exps(j, scaled, neg_z, tot):
+            bank = new_bank("zbank")
+            for b in range(L):
+                nc.tensor.transpose(bank[:, block(b)], scaled[b][:, block(j)], ident[:])
+            neg_max = work.tile([P, 1], F32, name="neg_max", tag="neg_max", bufs=4)
+            nc.vector.tensor_scalar(neg_z, bank[:], neg_us[:, j : j + 1], None, ALU.mult, ALU.min, accum_out=neg_max[:])
+            e = work.tile([P, N], F32, name="e", tag="e", bufs=8)
+            nc.scalar.activation(e[:], neg_z, ACT.Exp, bias=neg_max[:], scale=-1.0, accum_out=tot)
+            return e
+
+        def gradient(e, inv, y, c, scale_all, u, turned):
+            nc.vector.scalar_tensor_tensor(u, e[:], inv, y, ALU.mult, ALU.subtract)
+            g = work.tile([P, N], BF16, name="g", tag="g")
+            nc.vector.scalar_tensor_tensor(g[:], u, c, scale_all[:], ALU.mult, ALU.mult)
+            words = g[:].bitcast(F32)
+            bank = new_bank("turn")
+            for v in range(2):
+                nc.tensor.transpose(bank[:, block(v)], words[:, v : N // 2 : 2], ident[:])
+            nc.scalar.copy(
+                out=turned.bitcast(F32).rearrange("p (r v) -> p r v", v=2),
+                in_=bank[:, 0 : 2 * P].rearrange("p (v r) -> p r v", v=2),
+            )
+
+        head_scaled = [scores("head_scaled", b, hq, block(b), th_col) for b in range(L)]
+        h_rows = quantize("h_rows", h_turned[:], E4)
+
+        w_turned = kept("w_turned", [P, L * N], BF16)
+
+        def gather(t):
+            nc.vector.tensor_copy(arena[:, t * S : t * S + N], w_raw[t][:].indirect(offsets[:]))
+
+        def turn_w(b, tag):
+            bank = new_bank(tag)
+            for s in range(2):
+                t = 2 * b + s
+                words = arena[:, t * S : t * S + N].bitcast(F32)
+                for v in range(2):
+                    nc.tensor.transpose(bank[:, block(2 * s + v)], words[:, v : N // 2 : 2], ident[:])
+            nc.scalar.copy(
+                out=w_turned[:].bitcast(F32).rearrange("p (q b k) -> p b q k", b=2, k=L)[:, b],
+                in_=bank[:].rearrange("p (k q) -> p q k", k=L),
+            )
+
+        gather(0)
+        ts_row = arena[:, N : 3 * N].bitcast(F32)
+        nc.vector.tensor_copy(ts_row, ts_win[:].indirect(offsets[:]))
+        gather(1)
+
+        head_tot = kept("head_tot", [P, L], F32)
+        head_e = []
+        for j in range(L):
+            if j < 2:
+                neg_z = arena[:, (j + 2) * S : (j + 2) * S + 2 * N].bitcast(F32)
+            else:
+                neg_z = work.tile([P, N], F32, name="z", tag="z")[:]
+            head_e.append(exps(j, head_scaled, neg_z, head_tot[:, j : j + 1]))
+        gather(2)
+        gather(3)
+
+        bank = new_bank("acc")
+        for j in range(L):
+            nc.tensor.transpose(bank[:, block(j)], ts_row[:, block(j)], ident[:])
+        ts_col = kept("ts_col", [P, L], F32)
+        nc.scalar.copy(out=ts_col[:], in_=bank[:, 0:N:P])
+        th_all = spread("th_all", th_col)
+        ts_all = spread("ts_all", ts_col)
+        turn_w(0, "turn")
+
+        w_int = kept("w_int", [P, L * N], BF16)
+        tail_scaled = []
+        for b in range(L):
+            nc.vector.tensor_copy(
+                out=w_int[:, block(b, N)].rearrange("p (c i t) -> p c t i", i=L, t=L),
+                in_=arena[:].rearrange("p (t h b c i) -> p h b c t i", t=L, h=3, b=L, i=L)[:, 0, b],
+            )
+            if b:
+                tail_scaled.append(scores("tail_scaled", b - 1, quantize("w%d" % (b - 1), w_int[:, block(b - 1, N)], E4), block(0), ts_col))
+        tail_scaled.append(scores("tail_scaled", L - 1, quantize("w%d" % (L - 1), w_int[:, block(L - 1, N)], E4), block(0), ts_col))
+
+        head_inv = kept("head_inv", [P, L], F32)
+        nc.vector.reciprocal(head_inv[:], head_tot[:])
+        head_u = kept("head_u", [P, T], F32, tag="w_raw3")
+        head_turned = kept("head_turned", [P, L * N], BF16)
+
+        def head_gradient(j):
+            gradient(head_e[j], head_inv[:, j : j + 1], yh_rows[j], c_head[:, j : j + 1], th_all, head_u[:, block(j, N)], head_turned[:, block(j, N)])
+
+        tail_e, tail_tot = [], []
+        for j in range(L):
+            tail_tot.append(kept("tail_tot%d" % j, [P, 1], F32))
+            neg_z = work.tile([P, N], F32, name="z", tag="z")[:]
+            tail_e.append(exps(j, tail_scaled, neg_z, tail_tot[j][:]))
+            head_gradient(j)
+        turn_w(1, "zbank")
+        ghq = quantize("gh", head_turned[:], E5)
+        w_rows = quantize("w_rows", w_turned[:], E4)
+
+        result = kept("result", [P, L * N], F32)
+        out_rows = out_0.rearrange("(p j) d -> j p d", j=L)
+        for j in range(L):
+            inv = kept("tail_inv%d" % j, [P, 1], F32)
+            nc.vector.reciprocal(inv[:], tail_tot[j][:])
+            u = work.tile([P, N], F32, name="u", tag="u", bufs=2)
+            turned = work.tile([P, N], BF16, name="turned", tag="turned", align_bytes=64)
+            gradient(tail_e[j], inv[:], yt_rows[j], c_tail[:, j : j + 1], ts_all, u[:], turned[:])
+            gq = quantize("gt%d" % j, turned[:], E5)
+            bank = new_bank("acc")
+            mm(bank[:], ghq, E5, block(j), h_rows, True, False)
+            mm(bank[:], gq, E5, block(0), w_rows, False, True)
+            nc.scalar.copy(out=result[:, block(j, N)], in_=bank[:])
+            nc.sync.dma_start(out=out_rows[j], in_=result[:, block(j, N)])
+
+        out_bf = kept("out_bf", [P, L * N], BF16)
+        out_codes = kept("out_codes", [P, N], U32)
+        out_scales = kept("out_scales", [P, N], U8)
+        words_out = out_1.rearrange("o p c l -> p (o c l)").bitcast(I32)
+        H = N // 2
+        for a in range(2):
+            nc.vector.tensor_copy(
+                out=out_bf[:, block(a, L * H)].rearrange("p (c i t) -> p c t i", i=L, t=L),
+                in_=result[:].rearrange("p (t a c i) -> p a c t i", t=L, a=2, i=L)[:, a],
+            )
+        for a in range(2):
+            nc.vector.quantize_mx(
+                out=out_codes[:, block(a, H)].bitcast(E4),
+                scales=out_scales[:, block(a, H)],
+                in_=out_bf[:, block(a, L * H)],
+            )
+            nc.sync.dma_start(out=words_out[:, block(a, H)], in_=out_codes[:, block(a, H)].bitcast(I32))
+        scales_out = out_2.rearrange("o b c -> (o b) c").bitcast(I32)
+        for q in range(L):
+            queue = nc.scalar if q % 2 else nc.sync
+            queue.dma_start(out=scales_out[L * q : L * q + L, :], in_=out_scales[32 * q : 32 * q + L, :].bitcast(I32))

@@ -9,16 +9,30 @@ U32 = mybir.dt.uint32
 I32 = mybir.dt.int32
 U16 = mybir.dt.uint16
 U8 = mybir.dt.uint8
-E4 = mybir.dt.float8_e4m3fn_x4
-E5 = mybir.dt.float8_e5m2_x4
+E4M3 = mybir.dt.float8_e4m3fn_x4
+E5M2 = mybir.dt.float8_e5m2_x4
 ALU = mybir.AluOpType
 ACT = mybir.ActivationFunctionType
 
 P = 128
-L = 4
-N = 512
-T = 2048
+LANES = 4
+N = P * LANES
+TABLE = 2048
+BANKS = 8
 FLOPS = 4 * 2 * N * N * N
+BYTES = 4 * (5 * N * N + N * TABLE + TABLE + 4 * N) + 2 * P * N // 16 + N * N + 16 * N
+
+HEAD_SCORE_BANKS = (0, 1, 2, 3)
+HEAD_LOGIT_BANKS = (4, 5, 0, 1)
+TAIL_SCORE_BANKS = (2, 3, 4, 5)
+TAIL_LOGIT_BANKS = (0, 1, 2, 3)
+HEAD_GRADIENT_BANKS = (6, 4, 5, 6)
+TAIL_GRADIENT_BANKS = (6, 7, 6, 7)
+RESULT_BANKS = (4, 5, 0, 1)
+
+
+def block(n, width=P):
+    return slice(n * width, (n + 1) * width)
 
 
 def tile_attend_gadsm_x_pl_kernel(tc, xT, wT, hT, us, ts, th, wt, wh, yt, yh, offs, out_0, out_1, out_2):
@@ -26,254 +40,280 @@ def tile_attend_gadsm_x_pl_kernel(tc, xT, wT, hT, us, ts, th, wt, wh, yt, yh, of
     with ExitStack() as ctx:
         keep = ctx.enter_context(tc.tile_pool(name="keep", bufs=1))
         work = ctx.enter_context(tc.tile_pool(name="work", bufs=3))
-        psum = ctx.enter_context(tc.psum_pool(name="psum", bufs=2))
+        psum = ctx.enter_context(tc.psum_pool(name="psum", bufs=1))
+        banks = [psum.tile([P, N], F32, name="bank%d" % n) for n in range(BANKS)]
 
         def kept(name, shape, dtype, tag=None):
             return keep.tile(shape, dtype, name=name, tag=tag or name, align_bytes=64)
-
-        def block(j, width=P):
-            return slice(j * width, (j + 1) * width)
 
         ident = kept("ident", [P, P], F32)
         make_identity(nc, ident[:])
         warm = kept("warm", [P, 1], F32)
         nc.vector.memset(warm[:], 0.0)
         nc.scalar.activation(warm[:], warm[:], ACT.Exp)
-        h_raw = kept("h_raw", [P, L * N], F32)
-        nc.sync.dma_start(out=h_raw[:], in_=hT.rearrange("(p t) r -> p (t r)", t=L))
-        x_raw = kept("x_raw", [P, L * N], F32)
-        nc.sync.dma_start(out=x_raw[:], in_=xT.rearrange("(p t) r -> p (t r)", t=L))
 
+        ts_window = kept("ts_window", [P, TABLE], F32)
+        nc.vector.memset(ts_window[:], 0.0)
+        nc.scalar.dma_start(out=ts_window[0:1, :], in_=ts[0:1, :])
+        th_lanes = kept("th_lanes", [P, LANES], F32)
+        nc.sync.dma_start(out=th_lanes[:], in_=th[0:1, :].rearrange("o (p t) -> p (o t)", t=LANES))
+        h_raw = kept("h_raw", [P, LANES * N], F32)
+        nc.sync.dma_start(out=h_raw[:], in_=hT.rearrange("(p t) c -> p (t c)", t=LANES))
+        x_raw = kept("x_raw", [P, LANES * N], F32)
+        nc.sync.dma_start(out=x_raw[:], in_=xT.rearrange("(p t) c -> p (t c)", t=LANES))
         offsets = kept("offsets", [P, N // 16], U16)
         nc.sync.dma_start(offsets[:], offs)
-        ts_win = kept("ts_win", [P, T], F32)
-        nc.vector.memset(ts_win[:], 0.0)
-        th_col = kept("th_col", [P, L], F32)
-        with nc.allow_non_contiguous_dma(reason="one scale a partition"):
-            nc.sync.dma_start(out=th_col[:], in_=th[0:1, :].rearrange("o (j p) -> p (o j)", j=L))
-        cols = {}
-        for name, src in (("us", us), ("wh", wh), ("wt", wt)):
-            cols[name] = kept(name + "_col", [P, L], F32)
-            nc.sync.dma_start(out=cols[name][:], in_=src.rearrange("(p j) o -> p (j o)", j=L))
 
-        nc.scalar.dma_start(out=ts_win[0:1, :], in_=ts[0:1, :])
+        def load_row_factors(name, src):
+            factors = kept(name, [P, LANES], F32)
+            nc.sync.dma_start(out=factors[:], in_=src.rearrange("(q j) o -> q (j o)", j=LANES))
+            return factors
 
-        def load_targets(name, y):
-            halves = []
-            for a in range(2):
-                half = kept(name + "%d" % a, [P, 2 * N], F32)
-                nc.sync.dma_start(out=half[:], in_=y.rearrange("(p a j) i -> a p (j i)", a=2, j=2)[a])
-                halves.append(half)
-            return [halves[j // 2][:, block(j % 2, N)] for j in range(L)]
-
+        us_rows = load_row_factors("us_rows", us)
+        wh_rows = load_row_factors("wh_rows", wh)
+        wt_rows = load_row_factors("wt_rows", wt)
         w_raw = []
-        for t in range(L):
-            w_raw.append(kept("w_raw%d" % t, [P, T], F32))
-            nc.sync.dma_start(out=w_raw[t][:], in_=wT.rearrange("(p t) c -> t p c", t=L)[t])
-        yh_rows = load_targets("yh", yh)
-        yt_rows = load_targets("yt", yt)
+        for t in range(LANES):
+            w_raw.append(kept("w_raw%d" % t, [P, TABLE], F32))
+            nc.sync.dma_start(out=w_raw[t][:], in_=wT.rearrange("(p t) c -> t p c", t=LANES)[t])
 
+        def load_targets(name, src):
+            tiles = []
+            for a in range(2):
+                pair = kept(name + "%d" % a, [P, 2 * N], F32)
+                nc.sync.dma_start(out=pair[:], in_=src.rearrange("(q a j) c -> a q (j c)", a=2, j=2)[a])
+                tiles.extend([pair[:, block(0, N)], pair[:, block(1, N)]])
+            return tiles
 
-        def quantize(name, src, fmt):
-            width = src.shape[1] // L
-            codes = kept(name + "_codes", [P, width], U32)
-            scales = kept(name + "_scales", [P, width], U8)
-            nc.vector.quantize_mx(out=codes[:].bitcast(fmt), scales=scales[:], in_=src)
-            return codes, scales
+        yh_tiles = load_targets("yh", yh)
+        yt_tiles = load_targets("yt", yt)
 
-        def mm(out, lhs, lhs_fmt, lhs_cols, rhs, start, stop):
+        def mx_tiles(name, columns):
+            return kept(name + "_codes", [P, columns], U32), kept(name + "_scales", [P, columns], U8)
+
+        def quantize(mx, columns, src, fmt):
+            nc.vector.quantize_mx(out=mx[0][:, columns].bitcast(fmt), scales=mx[1][:, columns], in_=src)
+
+        def quantized(name, src, fmt):
+            columns = src.shape[1] // LANES
+            mx = mx_tiles(name, columns)
+            quantize(mx, slice(0, columns), src, fmt)
+            return mx
+
+        def multiply(bank, lhs, lhs_fmt, lhs_columns, rhs, start, stop):
             nc.tensor.matmul_mx(
-                out=out,
-                lhsT=lhs[0][:, lhs_cols].bitcast(lhs_fmt),
-                lhsT_scale=lhs[1][:, lhs_cols],
-                rhs=rhs[0][:].bitcast(E4),
+                out=bank[:],
+                lhsT=lhs[0][:, lhs_columns].bitcast(lhs_fmt),
+                lhsT_scale=lhs[1][:, lhs_columns],
+                rhs=rhs[0][:].bitcast(E4M3),
                 rhs_scale=rhs[1][:],
                 start=start,
                 stop=stop,
             )
 
-        def new_bank(tag):
-            return psum.tile([P, N], F32, name=tag, tag=tag)
-
-        h_bf = kept("h_bf", [P, L * N], BF16)
-        nc.vector.tensor_copy(
-            out=h_bf[:].rearrange("p (c i t) -> p c t i", i=L, t=L),
-            in_=h_raw[:].rearrange("p (t c i) -> p c t i", t=L, i=L),
-        )
-        hq = quantize("h", h_bf[:], E4)
-
-        S = 3 * N
-        arena = kept("arena", [P, L * S], BF16)
-        x_bf = arena[:, 0 : L * N]
-        nc.vector.tensor_copy(
-            out=x_bf.rearrange("p (j q t) -> p q t j", j=L, t=L),
-            in_=x_raw[:].rearrange("p (t q j) -> p q t j", t=L, j=L),
-        )
-        xq = quantize("x", x_bf, E4)
-
-        h_words = h_bf[:].bitcast(F32)
-        h_turned = kept("h_turned", [P, L * N], BF16)
-        for v in range(2):
-            bank = new_bank("score" if v == 0 else "zbank")
-            for t in range(L):
-                nc.tensor.transpose(bank[:, block(t)], h_words[:, 2 * t + v : 2 * N : 8], ident[:])
-            nc.scalar.copy(
-                out=h_turned[:].rearrange("q (p v e t) -> q v p e t", v=2, e=2, t=L)[:, v],
-                in_=bank[:].bitcast(BF16).rearrange("q (t p e) -> q p e t", t=L, e=2),
+        def interleave(copy, dst, lanes, part, parts):
+            copy(
+                out=dst[:, block(part, LANES * N // parts)].rearrange("p (c i t) -> p c t i", i=4, t=LANES),
+                in_=lanes[:, :, block(part, N // parts)].rearrange("p t (c i) -> p c t i", i=4),
             )
 
-        neg_us = kept("neg_us", [P, L], F32)
-        nc.gpsimd.tensor_scalar(neg_us[:], cols["us"][:], -1.0, 0.0, ALU.mult, ALU.add)
-        c_head = kept("c_head", [P, L], F32)
-        nc.gpsimd.tensor_tensor(c_head[:], cols["wh"][:], cols["us"][:], ALU.mult)
-        c_tail = kept("c_tail", [P, L], F32)
-        nc.gpsimd.tensor_tensor(c_tail[:], cols["wt"][:], cols["us"][:], ALU.mult)
+        def spread(bank, columns):
+            for n in range(LANES):
+                nc.tensor.transpose(bank[:, block(n)], columns[:, n : n + 1].to_broadcast([P, P]), ident[:])
 
-        def spread(name, col):
-            bank = new_bank("zbank")
-            for j in range(L):
-                nc.tensor.transpose(bank[:, block(j)], col[:, j : j + 1].to_broadcast([P, P]), ident[:])
-            rows = kept(name, [P, N], F32)
-            nc.scalar.copy(out=rows[:], in_=bank[:])
-            return rows
+        def to_columns(name, bank, rows):
+            for n in range(LANES):
+                nc.tensor.transpose(bank[:, block(n)], rows[:, block(n)], ident[:])
+            columns = kept(name, [P, LANES], F32)
+            nc.scalar.copy(out=columns[:], in_=bank[:, 0:N:P])
+            return columns
 
-        def scores(name, b, lhs, lhs_cols, col):
-            bank = new_bank("score")
-            mm(bank[:], lhs, E4, lhs_cols, xq, True, True)
-            scaled = kept(name + "%d" % b, [P, N], F32)
-            nc.scalar.activation(scaled[:], bank[:], ACT.Copy, scale=col[:, b : b + 1])
+        def along_d(name, raw, rounded):
+            mx = mx_tiles(name, N)
+            for half in range(2):
+                interleave(nc.vector.tensor_copy, rounded, raw[:].rearrange("p (t c) -> p t c", t=LANES), half, 2)
+            for half in range(2):
+                quantize(mx, block(half, N // 2), rounded[:, block(half, 2 * N)], E4M3)
+            return mx
+
+        def scores(name, bank, words, columns, scale):
+            multiply(bank, words, E4M3, columns, x_mx, True, True)
+            scaled = kept(name, [P, N], F32)
+            nc.scalar.activation(
+                scaled[:].rearrange("p (j q) -> p j q", j=LANES),
+                bank[:].rearrange("p (q j) -> p j q", j=LANES),
+                ACT.Copy,
+                scale=scale,
+            )
             return scaled
 
-        def exps(j, scaled, neg_z, tot):
-            bank = new_bank("zbank")
-            for b in range(L):
-                nc.tensor.transpose(bank[:, block(b)], scaled[b][:, block(j)], ident[:])
-            neg_max = work.tile([P, 1], F32, name="neg_max", tag="neg_max", bufs=4)
+        def exponentials(j, bank, scaled, neg_z, total):
+            for n in range(LANES):
+                nc.tensor.transpose(bank[:, block(n)], scaled[n][:, block(j)], ident[:])
+            neg_max = work.tile([P, 1], F32, name="neg_max", bufs=LANES)
             nc.vector.tensor_scalar(neg_z, bank[:], neg_us[:, j : j + 1], None, ALU.mult, ALU.min, accum_out=neg_max[:])
-            e = work.tile([P, N], F32, name="e", tag="e", bufs=8)
-            nc.scalar.activation(e[:], neg_z, ACT.Exp, bias=neg_max[:], scale=-1.0, accum_out=tot)
+            e = work.tile([P, N], F32, name="e", bufs=2 * LANES)
+            nc.scalar.activation(e[:], neg_z, ACT.Exp, bias=neg_max[:], scale=-1.0, accum_out=total)
             return e
 
-        def gradient(e, inv, y, c, scale_all, u, turned):
-            nc.vector.scalar_tensor_tensor(u, e[:], inv, y, ALU.mult, ALU.subtract)
-            g = work.tile([P, N], BF16, name="g", tag="g")
-            nc.vector.scalar_tensor_tensor(g[:], u, c, scale_all[:], ALU.mult, ALU.mult)
-            words = g[:].bitcast(F32)
-            bank = new_bank("turn")
+        def gradient(bank, e, inverse, targets, weight, word_scales, diff, turned):
+            nc.vector.scalar_tensor_tensor(diff, e[:], inverse, targets, ALU.mult, ALU.subtract)
+            g = work.tile([P, N], BF16, name="g")
+            nc.vector.scalar_tensor_tensor(g[:], diff, weight, word_scales[:], ALU.mult, ALU.mult)
+            pairs = g[:].bitcast(F32)
             for v in range(2):
-                nc.tensor.transpose(bank[:, block(v)], words[:, v : N // 2 : 2], ident[:])
+                nc.tensor.transpose(bank[:, block(v)], pairs[:, v : N // 2 : 2], ident[:])
             nc.scalar.copy(
-                out=turned.bitcast(F32).rearrange("p (r v) -> p r v", v=2),
-                in_=bank[:, 0 : 2 * P].rearrange("p (v r) -> p r v", v=2),
+                out=turned.bitcast(F32).rearrange("p (q v) -> p q v", v=2),
+                in_=bank[:, 0 : 2 * P].rearrange("p (v q) -> p q v", v=2),
             )
 
-        head_scaled = [scores("head_scaled", b, hq, block(b), th_col) for b in range(L)]
-        h_rows = quantize("h_rows", h_turned[:], E4)
+        th_rows = kept("th_rows", [P, N], F32)
+        spread(banks[0], th_lanes)
+        nc.scalar.copy(
+            out=th_rows[:].rearrange("m (p t) -> m p t", t=LANES),
+            in_=banks[0][:].rearrange("m (t p) -> m p t", t=LANES),
+        )
+        th_columns = to_columns("th_columns", banks[1], th_rows)
 
-        w_turned = kept("w_turned", [P, L * N], BF16)
+        h_rounded = kept("h_rounded", [P, LANES * N], BF16)
+        h_mx = along_d("h", h_raw, h_rounded[:])
+        PITCH = 3 * N
+        shared = kept("shared", [P, LANES * PITCH], BF16)
+        x_mx = along_d("x", x_raw, shared[:, 0 : LANES * N])
+
+        h_turned = kept("h_turned", [P, LANES * N], BF16)
+        h_pairs = h_rounded[:].bitcast(F32)
+        for v in range(2):
+            bank = banks[2 + v]
+            for t in range(LANES):
+                nc.tensor.transpose(bank[:, block(t)], h_pairs[:, 2 * t + v : 2 * N : 2 * LANES], ident[:])
+            nc.scalar.copy(
+                out=h_turned[:].rearrange("q (p v s t) -> q v p s t", v=2, s=2, t=LANES)[:, v],
+                in_=bank[:].bitcast(BF16).rearrange("q (t p s) -> q p s t", t=LANES, s=2),
+            )
+
+        neg_us = kept("neg_us", [P, LANES], F32)
+        nc.gpsimd.tensor_scalar(neg_us[:], us_rows[:], -1.0, 0.0, ALU.mult, ALU.add)
+        head_weight = kept("head_weight", [P, LANES], F32)
+        nc.gpsimd.tensor_tensor(head_weight[:], wh_rows[:], us_rows[:], ALU.mult)
+        tail_weight = kept("tail_weight", [P, LANES], F32)
+        nc.gpsimd.tensor_tensor(tail_weight[:], wt_rows[:], us_rows[:], ALU.mult)
+
+        def gathered(t):
+            return shared[:, t * PITCH : t * PITCH + N]
 
         def gather(t):
-            nc.vector.tensor_copy(arena[:, t * S : t * S + N], w_raw[t][:].indirect(offsets[:]))
+            nc.vector.tensor_copy(gathered(t), w_raw[t][:].indirect(offsets[:]))
 
-        def turn_w(b, tag):
-            bank = new_bank(tag)
-            for s in range(2):
-                t = 2 * b + s
-                words = arena[:, t * S : t * S + N].bitcast(F32)
-                for v in range(2):
-                    nc.tensor.transpose(bank[:, block(2 * s + v)], words[:, v : N // 2 : 2], ident[:])
-            nc.scalar.copy(
-                out=w_turned[:].bitcast(F32).rearrange("p (q b k) -> p b q k", b=2, k=L)[:, b],
-                in_=bank[:].rearrange("p (k q) -> p q k", k=L),
-            )
-
+        head_scaled = [
+            scores("head_scaled%d" % n, banks[HEAD_SCORE_BANKS[n]], h_mx, block(n), th_columns[:, n : n + 1]) for n in range(LANES)
+        ]
+        h_rows_mx = quantized("h_rows", h_turned[:], E4M3)
         gather(0)
-        ts_row = arena[:, N : 3 * N].bitcast(F32)
-        nc.vector.tensor_copy(ts_row, ts_win[:].indirect(offsets[:]))
+        ts_listed = shared[:, N : 3 * N].bitcast(F32)
+        nc.vector.tensor_copy(ts_listed, ts_window[:].indirect(offsets[:]))
         gather(1)
 
-        head_tot = kept("head_tot", [P, L], F32)
-        head_e = []
-        for j in range(L):
+        head_diff = kept("head_diff", [P, TABLE], F32, tag="w_raw%d" % (LANES - 1))
+        head_total = kept("head_total", [P, LANES], F32)
+
+        def head_exponentials(j):
             if j < 2:
-                neg_z = arena[:, (j + 2) * S : (j + 2) * S + 2 * N].bitcast(F32)
+                neg_z = shared[:, (j + 2) * PITCH : (j + 2) * PITCH + 2 * N].bitcast(F32)
             else:
-                neg_z = work.tile([P, N], F32, name="z", tag="z")[:]
-            head_e.append(exps(j, head_scaled, neg_z, head_tot[:, j : j + 1]))
+                neg_z = head_diff[:, block(j, N)]
+            return exponentials(j, banks[HEAD_LOGIT_BANKS[j]], head_scaled, neg_z, head_total[:, j : j + 1])
+
+        w_turned = kept("w_turned", [P, LANES * N], BF16)
+
+        def turn_gathered(bank, a):
+            for s in (1, 0):
+                pairs = gathered(2 * a + s).bitcast(F32)
+                for v in range(2):
+                    nc.tensor.transpose(bank[:, block(2 * s + v)], pairs[:, v : N // 2 : 2], ident[:])
+            nc.scalar.copy(
+                out=w_turned[:].bitcast(F32).rearrange("p (q a n) -> p a q n", a=2, n=4)[:, a],
+                in_=bank[:].rearrange("p (n q) -> p q n", n=4),
+            )
+
+        head_e = [head_exponentials(0), head_exponentials(1)]
         gather(2)
         gather(3)
+        ts_columns = to_columns("ts_columns", banks[3], ts_listed)
+        turn_gathered(banks[4], 0)
+        ts_rows = kept("ts_rows", [P, N], F32)
+        spread(banks[5], ts_columns)
+        nc.scalar.copy(out=ts_rows[:], in_=banks[5][:])
 
-        bank = new_bank("acc")
-        for j in range(L):
-            nc.tensor.transpose(bank[:, block(j)], ts_row[:, block(j)], ident[:])
-        ts_col = kept("ts_col", [P, L], F32)
-        nc.scalar.copy(out=ts_col[:], in_=bank[:, 0:N:P])
-        th_all = spread("th_all", th_col)
-        ts_all = spread("ts_all", ts_col)
-        turn_w(0, "turn")
+        w_rounded = kept("w_rounded", [P, LANES * N], BF16)
+        w_lanes = shared[:].rearrange("p (t c) -> p t c", t=LANES)[:, :, 0:N]
+        w_mx = []
+        for n in range(LANES + 1):
+            if n < LANES:
+                interleave(nc.scalar.copy, w_rounded[:], w_lanes, n, LANES)
+            if n > 0:
+                w_mx.append(quantized("w%d" % (n - 1), w_rounded[:, block(n - 1, N)], E4M3))
+        head_e.extend([head_exponentials(2), head_exponentials(3)])
+        tail_scaled = [
+            scores("tail_scaled%d" % n, banks[TAIL_SCORE_BANKS[n]], w_mx[n], block(0), ts_columns[:, n : n + 1]) for n in range(LANES)
+        ]
+        turn_gathered(banks[7], 1)
 
-        w_int = kept("w_int", [P, L * N], BF16)
-        tail_scaled = []
-        for b in range(L):
-            nc.vector.tensor_copy(
-                out=w_int[:, block(b, N)].rearrange("p (c i t) -> p c t i", i=L, t=L),
-                in_=arena[:].rearrange("p (t h b c i) -> p h b c t i", t=L, h=3, b=L, i=L)[:, 0, b],
+        head_inverse = kept("head_inverse", [P, LANES], F32)
+        gh_turned = kept("gh_turned", [P, LANES * N], BF16)
+        for j in range(LANES):
+            if j % 2 == 0:
+                nc.vector.reciprocal(head_inverse[:, j : j + 2], head_total[:, j : j + 2])
+            gradient(
+                banks[HEAD_GRADIENT_BANKS[j]],
+                head_e[j],
+                head_inverse[:, j : j + 1],
+                yh_tiles[j],
+                head_weight[:, j : j + 1],
+                th_rows,
+                head_diff[:, block(j, N)],
+                gh_turned[:, block(j, N)],
             )
-            if b:
-                tail_scaled.append(scores("tail_scaled", b - 1, quantize("w%d" % (b - 1), w_int[:, block(b - 1, N)], E4), block(0), ts_col))
-        tail_scaled.append(scores("tail_scaled", L - 1, quantize("w%d" % (L - 1), w_int[:, block(L - 1, N)], E4), block(0), ts_col))
+        gh_mx = quantized("gh", gh_turned[:], E5M2)
+        w_rows_mx = quantized("w_rows", w_turned[:], E4M3)
 
-        head_inv = kept("head_inv", [P, L], F32)
-        nc.vector.reciprocal(head_inv[:], head_tot[:])
-        head_u = kept("head_u", [P, T], F32, tag="w_raw3")
-        head_turned = kept("head_turned", [P, L * N], BF16)
+        tail_total, tail_e = [], []
+        for j in range(LANES):
+            tail_total.append(kept("tail_total%d" % j, [P, 1], F32))
+            neg_z = work.tile([P, N], F32, name="neg_z")
+            tail_e.append(exponentials(j, banks[TAIL_LOGIT_BANKS[j]], tail_scaled, neg_z[:], tail_total[j][:]))
 
-        def head_gradient(j):
-            gradient(head_e[j], head_inv[:, j : j + 1], yh_rows[j], c_head[:, j : j + 1], th_all, head_u[:, block(j, N)], head_turned[:, block(j, N)])
+        result = kept("result", [P, LANES * N], F32)
+        out_tiles = out_0.rearrange("(q j) d -> j q d", j=LANES)
+        for j in range(LANES):
+            inverse = kept("tail_inverse%d" % j, [P, 1], F32)
+            nc.vector.reciprocal(inverse[:], tail_total[j][:])
+            diff = work.tile([P, N], F32, name="diff", bufs=2)
+            g_turned = work.tile([P, N], BF16, name="g_turned", align_bytes=64)
+            gradient(banks[TAIL_GRADIENT_BANKS[j]], tail_e[j], inverse[:], yt_tiles[j], tail_weight[:, j : j + 1], ts_rows, diff[:], g_turned[:])
+            g_mx = quantized("g%d" % j, g_turned[:], E5M2)
+            bank = banks[RESULT_BANKS[j]]
+            multiply(bank, gh_mx, E5M2, block(j), h_rows_mx, True, False)
+            multiply(bank, g_mx, E5M2, block(0), w_rows_mx, False, True)
+            parts = 2 if j == LANES - 1 else 1
+            for part in range(parts):
+                columns = block(part, N // parts)
+                nc.scalar.copy(out=result[:, block(j, N)][:, columns], in_=bank[:, columns])
+            nc.sync.dma_start(out=out_tiles[j], in_=result[:, block(j, N)])
 
-        tail_e, tail_tot = [], []
-        for j in range(L):
-            tail_tot.append(kept("tail_tot%d" % j, [P, 1], F32))
-            neg_z = work.tile([P, N], F32, name="z", tag="z")[:]
-            tail_e.append(exps(j, tail_scaled, neg_z, tail_tot[j][:]))
-            head_gradient(j)
-        turn_w(1, "zbank")
-        ghq = quantize("gh", head_turned[:], E5)
-        w_rows = quantize("w_rows", w_turned[:], E4)
-
-        result = kept("result", [P, L * N], F32)
-        out_rows = out_0.rearrange("(p j) d -> j p d", j=L)
-        for j in range(L):
-            inv = kept("tail_inv%d" % j, [P, 1], F32)
-            nc.vector.reciprocal(inv[:], tail_tot[j][:])
-            u = work.tile([P, N], F32, name="u", tag="u", bufs=2)
-            turned = work.tile([P, N], BF16, name="turned", tag="turned", align_bytes=64)
-            gradient(tail_e[j], inv[:], yt_rows[j], c_tail[:, j : j + 1], ts_all, u[:], turned[:])
-            gq = quantize("gt%d" % j, turned[:], E5)
-            bank = new_bank("acc")
-            mm(bank[:], ghq, E5, block(j), h_rows, True, False)
-            mm(bank[:], gq, E5, block(0), w_rows, False, True)
-            nc.scalar.copy(out=result[:, block(j, N)], in_=bank[:])
-            nc.sync.dma_start(out=out_rows[j], in_=result[:, block(j, N)])
-
-        out_bf = kept("out_bf", [P, L * N], BF16)
-        out_codes = kept("out_codes", [P, N], U32)
-        out_scales = kept("out_scales", [P, N], U8)
-        words_out = out_1.rearrange("o p c l -> p (o c l)").bitcast(I32)
-        H = N // 2
-        for a in range(2):
-            nc.vector.tensor_copy(
-                out=out_bf[:, block(a, L * H)].rearrange("p (c i t) -> p c t i", i=L, t=L),
-                in_=result[:].rearrange("p (t a c i) -> p a c t i", t=L, a=2, i=L)[:, a],
-            )
-        for a in range(2):
-            nc.vector.quantize_mx(
-                out=out_codes[:, block(a, H)].bitcast(E4),
-                scales=out_scales[:, block(a, H)],
-                in_=out_bf[:, block(a, L * H)],
-            )
-            nc.sync.dma_start(out=words_out[:, block(a, H)], in_=out_codes[:, block(a, H)].bitcast(I32))
+        out_rounded = kept("out_rounded", [P, LANES * N], BF16)
+        out_mx = mx_tiles("out", N)
+        result_lanes = result[:].rearrange("p (t c) -> p t c", t=LANES)
+        interleave(nc.vector.tensor_copy, out_rounded[:], result_lanes, 0, 2)
+        interleave(nc.vector.tensor_copy, out_rounded[:], result_lanes, 2, 4)
+        interleave(nc.scalar.copy, out_rounded[:], result_lanes, 3, 4)
+        words_out = out_1.rearrange("o p c t -> p (o c t)").bitcast(I32)
+        for half in range(2):
+            columns = block(half, N // 2)
+            quantize(out_mx, columns, out_rounded[:, block(half, 2 * N)], E4M3)
+            nc.sync.dma_start(out=words_out[:, columns], in_=out_mx[0][:, columns].bitcast(I32))
         scales_out = out_2.rearrange("o b c -> (o b) c").bitcast(I32)
-        for q in range(L):
-            queue = nc.scalar if q % 2 else nc.sync
-            queue.dma_start(out=scales_out[L * q : L * q + L, :], in_=out_scales[32 * q : 32 * q + L, :].bitcast(I32))
+        for n in range(4):
+            queue = nc.scalar if n % 2 else nc.sync
+            queue.dma_start(out=scales_out[block(n, 4), :], in_=out_mx[1][32 * n : 32 * n + 4, :].bitcast(I32))

@@ -29,6 +29,7 @@ TAIL_LOGIT_BANKS = (0, 1, 2, 3)
 HEAD_GRADIENT_BANKS = (6, 4, 5, 6)
 TAIL_GRADIENT_BANKS = (6, 7, 6, 7)
 RESULT_BANKS = (4, 5, 0, 1)
+FINISH_LAG = 2
 
 
 def block(n, width=P):
@@ -147,19 +148,26 @@ def tile_attend_gadsm_x_pl_kernel(tc, xT, wT, hT, us, ts, th, wt, wh, yt, yh, of
             )
             return scaled
 
-        def exponentials(j, bank, scaled, neg_z, total):
+        def exponentials(j, bank, scaled, neg_scale, neg_z, total):
             for n in range(LANES):
                 nc.tensor.transpose(bank[:, block(n)], scaled[n][:, block(j)], ident[:])
             neg_max = work.tile([P, 1], F32, name="neg_max", bufs=LANES)
-            nc.vector.tensor_scalar(neg_z, bank[:], neg_us[:, j : j + 1], None, ALU.mult, ALU.min, accum_out=neg_max[:])
+            nc.vector.tensor_scalar(neg_z, bank[:], neg_scale[:, j : j + 1], None, ALU.mult, ALU.min, accum_out=neg_max[:])
             e = work.tile([P, N], F32, name="e", bufs=2 * LANES)
             nc.scalar.activation(e[:], neg_z, ACT.Exp, bias=neg_max[:], scale=-1.0, accum_out=total)
             return e
 
-        def gradient(bank, e, inverse, targets, weight, word_scales, diff, turned):
-            nc.vector.scalar_tensor_tensor(diff, e[:], inverse, targets, ALU.mult, ALU.subtract)
+        def row_factors(name, total, neg_weight, a):
+            inverse = kept(name + "_inverse%d" % a, [P, 2], F32)
+            nc.vector.reciprocal(inverse[:], total[:, block(a, 2)])
+            factor = kept(name + "_factor%d" % a, [P, 2], F32)
+            nc.vector.tensor_tensor(factor[:], inverse[:], neg_weight[:, block(a, 2)], ALU.mult)
+            return [factor[:, 0:1], factor[:, 1:2]]
+
+        def gradient(bank, e, total, targets, factor, word_scales, diff, turned):
+            nc.vector.scalar_tensor_tensor(diff, targets, total, e[:], ALU.mult, ALU.subtract)
             g = work.tile([P, N], BF16, name="g")
-            nc.vector.scalar_tensor_tensor(g[:], diff, weight, word_scales[:], ALU.mult, ALU.mult)
+            nc.vector.scalar_tensor_tensor(g[:], diff, factor, word_scales[:], ALU.mult, ALU.mult)
             pairs = g[:].bitcast(F32)
             for v in range(2):
                 nc.tensor.transpose(bank[:, block(v)], pairs[:, v : N // 2 : 2], ident[:])
@@ -195,10 +203,12 @@ def tile_attend_gadsm_x_pl_kernel(tc, xT, wT, hT, us, ts, th, wt, wh, yt, yh, of
 
         neg_us = kept("neg_us", [P, LANES], F32)
         nc.gpsimd.tensor_scalar(neg_us[:], us_rows[:], -1.0, 0.0, ALU.mult, ALU.add)
-        head_weight = kept("head_weight", [P, LANES], F32)
-        nc.gpsimd.tensor_tensor(head_weight[:], wh_rows[:], us_rows[:], ALU.mult)
-        tail_weight = kept("tail_weight", [P, LANES], F32)
-        nc.gpsimd.tensor_tensor(tail_weight[:], wt_rows[:], us_rows[:], ALU.mult)
+        neg_us_early = shared[:, 3 * PITCH : 3 * PITCH + 2 * LANES].bitcast(F32)
+        nc.gpsimd.tensor_scalar(neg_us_early, us_rows[:], -1.0, 0.0, ALU.mult, ALU.add)
+        neg_head_weight = kept("neg_head_weight", [P, LANES], F32)
+        nc.gpsimd.tensor_tensor(neg_head_weight[:], wh_rows[:], neg_us[:], ALU.mult)
+        neg_tail_weight = kept("neg_tail_weight", [P, LANES], F32)
+        nc.gpsimd.tensor_tensor(neg_tail_weight[:], wt_rows[:], neg_us[:], ALU.mult)
 
         def gathered(t):
             return shared[:, t * PITCH : t * PITCH + N]
@@ -220,10 +230,10 @@ def tile_attend_gadsm_x_pl_kernel(tc, xT, wT, hT, us, ts, th, wt, wh, yt, yh, of
 
         def head_exponentials(j):
             if j < 2:
-                neg_z = shared[:, (j + 2) * PITCH : (j + 2) * PITCH + 2 * N].bitcast(F32)
+                neg_scale, neg_z = neg_us_early, work.tile([P, N], F32, name="neg_z")[:]
             else:
-                neg_z = head_diff[:, block(j, N)]
-            return exponentials(j, banks[HEAD_LOGIT_BANKS[j]], head_scaled, neg_z, head_total[:, j : j + 1])
+                neg_scale, neg_z = neg_us, head_diff[:, block(j, N)]
+            return exponentials(j, banks[HEAD_LOGIT_BANKS[j]], head_scaled, neg_scale, neg_z, head_total[:, j : j + 1])
 
         w_turned = kept("w_turned", [P, LANES * N], BF16)
 
@@ -251,7 +261,7 @@ def tile_attend_gadsm_x_pl_kernel(tc, xT, wT, hT, us, ts, th, wt, wh, yt, yh, of
         w_mx = []
         for n in range(LANES + 1):
             if n < LANES:
-                interleave(nc.scalar.copy, w_rounded[:], w_lanes, n, LANES)
+                interleave(nc.vector.tensor_copy if n < LANES // 2 else nc.scalar.copy, w_rounded[:], w_lanes, n, LANES)
             if n > 0:
                 w_mx.append(quantized("w%d" % (n - 1), w_rounded[:, block(n - 1, N)], E4M3))
         head_e.extend([head_exponentials(2), head_exponentials(3)])
@@ -260,17 +270,17 @@ def tile_attend_gadsm_x_pl_kernel(tc, xT, wT, hT, us, ts, th, wt, wh, yt, yh, of
         ]
         turn_gathered(banks[7], 1)
 
-        head_inverse = kept("head_inverse", [P, LANES], F32)
+        head_factor = []
         gh_turned = kept("gh_turned", [P, LANES * N], BF16)
         for j in range(LANES):
             if j % 2 == 0:
-                nc.vector.reciprocal(head_inverse[:, j : j + 2], head_total[:, j : j + 2])
+                head_factor.extend(row_factors("head", head_total, neg_head_weight, j // 2))
             gradient(
                 banks[HEAD_GRADIENT_BANKS[j]],
                 head_e[j],
-                head_inverse[:, j : j + 1],
+                head_total[:, j : j + 1],
                 yh_tiles[j],
-                head_weight[:, j : j + 1],
+                head_factor[j],
                 th_rows,
                 head_diff[:, block(j, N)],
                 gh_turned[:, block(j, N)],
@@ -278,21 +288,34 @@ def tile_attend_gadsm_x_pl_kernel(tc, xT, wT, hT, us, ts, th, wt, wh, yt, yh, of
         gh_mx = quantized("gh", gh_turned[:], E5M2)
         w_rows_mx = quantized("w_rows", w_turned[:], E4M3)
 
-        tail_total, tail_e = [], []
+        tail_total = kept("tail_total", [P, LANES], F32)
+        tail_e = []
         for j in range(LANES):
-            tail_total.append(kept("tail_total%d" % j, [P, 1], F32))
             neg_z = work.tile([P, N], F32, name="neg_z")
-            tail_e.append(exponentials(j, banks[TAIL_LOGIT_BANKS[j]], tail_scaled, neg_z[:], tail_total[j][:]))
+            tail_e.append(exponentials(j, banks[TAIL_LOGIT_BANKS[j]], tail_scaled, neg_us, neg_z[:], tail_total[:, j : j + 1]))
 
         result = kept("result", [P, LANES * N], F32)
         out_tiles = out_0.rearrange("(q j) d -> j q d", j=LANES)
-        for j in range(LANES):
-            inverse = kept("tail_inverse%d" % j, [P, 1], F32)
-            nc.vector.reciprocal(inverse[:], tail_total[j][:])
+        g_turned = [kept("g_turned%d" % j, [P, N], BF16) for j in range(LANES)]
+        tail_factor = []
+
+        def tail_gradient(j):
+            if j % 2 == 0:
+                tail_factor.extend(row_factors("tail", tail_total, neg_tail_weight, j // 2))
             diff = work.tile([P, N], F32, name="diff", bufs=2)
-            g_turned = work.tile([P, N], BF16, name="g_turned", align_bytes=64)
-            gradient(banks[TAIL_GRADIENT_BANKS[j]], tail_e[j], inverse[:], yt_tiles[j], tail_weight[:, j : j + 1], ts_rows, diff[:], g_turned[:])
-            g_mx = quantized("g%d" % j, g_turned[:], E5M2)
+            gradient(
+                banks[TAIL_GRADIENT_BANKS[j]],
+                tail_e[j],
+                tail_total[:, j : j + 1],
+                yt_tiles[j],
+                tail_factor[j],
+                ts_rows,
+                diff[:],
+                g_turned[j][:],
+            )
+
+        def finish(j):
+            g_mx = quantized("g%d" % j, g_turned[j][:], E5M2)
             bank = banks[RESULT_BANKS[j]]
             multiply(bank, gh_mx, E5M2, block(j), h_rows_mx, True, False)
             multiply(bank, g_mx, E5M2, block(0), w_rows_mx, False, True)
@@ -301,6 +324,12 @@ def tile_attend_gadsm_x_pl_kernel(tc, xT, wT, hT, us, ts, th, wt, wh, yt, yh, of
                 columns = block(part, N // parts)
                 nc.scalar.copy(out=result[:, block(j, N)][:, columns], in_=bank[:, columns])
             nc.sync.dma_start(out=out_tiles[j], in_=result[:, block(j, N)])
+
+        for j in range(LANES + FINISH_LAG):
+            if j < LANES:
+                tail_gradient(j)
+            if j >= FINISH_LAG:
+                finish(j - FINISH_LAG)
 
         out_rounded = kept("out_rounded", [P, LANES * N], BF16)
         out_mx = mx_tiles("out", N)

@@ -58,10 +58,16 @@ def tile_attend_gadsm_x_pl_kernel(tc, xT, wT, hT, us, ts, th, wt, wh, yt, yh, of
         nc.scalar.dma_start(out=ts_window[0:1, :], in_=ts[0:1, :])
         th_lanes = kept("th_lanes", [P, LANES], F32)
         nc.sync.dma_start(out=th_lanes[:], in_=th[0:1, :].rearrange("o (p t) -> p (o t)", t=LANES))
-        h_raw = kept("h_raw", [P, LANES * N], F32)
-        nc.sync.dma_start(out=h_raw[:], in_=hT.rearrange("(p t) c -> p (t c)", t=LANES))
-        x_raw = kept("x_raw", [P, LANES * N], F32)
-        nc.sync.dma_start(out=x_raw[:], in_=xT.rearrange("(p t) c -> p (t c)", t=LANES))
+
+        def load_halves(name, src):
+            raw = kept(name, [P, LANES * N], F32)
+            halves = [raw[:, block(a, 2 * N)].rearrange("p (t c) -> p t c", t=LANES) for a in range(2)]
+            for a in range(2):
+                nc.sync.dma_start(out=halves[a], in_=src.rearrange("(p t) c -> p t c", t=LANES)[:, :, block(a, N // 2)])
+            return halves
+
+        h_halves = load_halves("h_raw", hT)
+        x_halves = load_halves("x_raw", xT)
         offsets = kept("offsets", [P, N // 16], U16)
         nc.sync.dma_start(offsets[:], offs)
 
@@ -112,10 +118,10 @@ def tile_attend_gadsm_x_pl_kernel(tc, xT, wT, hT, us, ts, th, wt, wh, yt, yh, of
                 stop=stop,
             )
 
-        def interleave(copy, dst, lanes, part, parts):
+        def interleave(copy, dst, lanes):
             copy(
-                out=dst[:, block(part, LANES * N // parts)].rearrange("p (c i t) -> p c t i", i=4, t=LANES),
-                in_=lanes[:, :, block(part, N // parts)].rearrange("p t (c i) -> p c t i", i=4),
+                out=dst.rearrange("p (c i t) -> p c t i", i=4, t=LANES),
+                in_=lanes.rearrange("p t (c i) -> p c t i", i=4),
             )
 
         def spread(bank, columns):
@@ -129,12 +135,12 @@ def tile_attend_gadsm_x_pl_kernel(tc, xT, wT, hT, us, ts, th, wt, wh, yt, yh, of
             nc.scalar.copy(out=columns[:], in_=bank[:, 0:N:P])
             return columns
 
-        def along_d(name, raw, rounded):
+        def along_d(name, halves, rounded):
             mx = mx_tiles(name, N)
-            for half in range(2):
-                interleave(nc.vector.tensor_copy, rounded, raw[:].rearrange("p (t c) -> p t c", t=LANES), half, 2)
-            for half in range(2):
-                quantize(mx, block(half, N // 2), rounded[:, block(half, 2 * N)], E4M3)
+            for a in range(2):
+                interleave(nc.vector.tensor_copy, rounded[:, block(a, 2 * N)], halves[a])
+            for a in range(2):
+                quantize(mx, block(a, N // 2), rounded[:, block(a, 2 * N)], E4M3)
             return mx
 
         def scores(name, bank, words, columns, scale):
@@ -185,10 +191,10 @@ def tile_attend_gadsm_x_pl_kernel(tc, xT, wT, hT, us, ts, th, wt, wh, yt, yh, of
         th_columns = to_columns("th_columns", banks[1], th_rows)
 
         h_rounded = kept("h_rounded", [P, LANES * N], BF16)
-        h_mx = along_d("h", h_raw, h_rounded[:])
+        h_mx = along_d("h", h_halves, h_rounded[:])
         PITCH = 3 * N
         shared = kept("shared", [P, LANES * PITCH], BF16)
-        x_mx = along_d("x", x_raw, shared[:, 0 : LANES * N])
+        x_mx = along_d("x", x_halves, shared[:, 0 : LANES * N])
 
         h_turned = kept("h_turned", [P, LANES * N], BF16)
         h_pairs = h_rounded[:].bitcast(F32)
@@ -203,8 +209,9 @@ def tile_attend_gadsm_x_pl_kernel(tc, xT, wT, hT, us, ts, th, wt, wh, yt, yh, of
 
         neg_us = kept("neg_us", [P, LANES], F32)
         nc.gpsimd.tensor_scalar(neg_us[:], us_rows[:], -1.0, 0.0, ALU.mult, ALU.add)
-        neg_us_early = shared[:, 3 * PITCH : 3 * PITCH + 2 * LANES].bitcast(F32)
-        nc.gpsimd.tensor_scalar(neg_us_early, us_rows[:], -1.0, 0.0, ALU.mult, ALU.add)
+        neg_us_in_lane = {t: shared[:, t * PITCH : t * PITCH + 2 * LANES].bitcast(F32) for t in (2, 3)}
+        for t in (3, 2):
+            nc.gpsimd.tensor_scalar(neg_us_in_lane[t], us_rows[:], -1.0, 0.0, ALU.mult, ALU.add)
         neg_head_weight = kept("neg_head_weight", [P, LANES], F32)
         nc.gpsimd.tensor_tensor(neg_head_weight[:], wh_rows[:], neg_us[:], ALU.mult)
         neg_tail_weight = kept("neg_tail_weight", [P, LANES], F32)
@@ -220,17 +227,17 @@ def tile_attend_gadsm_x_pl_kernel(tc, xT, wT, hT, us, ts, th, wt, wh, yt, yh, of
             scores("head_scaled%d" % n, banks[HEAD_SCORE_BANKS[n]], h_mx, block(n), th_columns[:, n : n + 1]) for n in range(LANES)
         ]
         h_rows_mx = quantized("h_rows", h_turned[:], E4M3)
-        gather(0)
         ts_listed = shared[:, N : 3 * N].bitcast(F32)
         nc.vector.tensor_copy(ts_listed, ts_window[:].indirect(offsets[:]))
+        gather(0)
         gather(1)
 
         head_diff = kept("head_diff", [P, TABLE], F32, tag="w_raw%d" % (LANES - 1))
         head_total = kept("head_total", [P, LANES], F32)
 
         def head_exponentials(j):
-            if j < 2:
-                neg_scale, neg_z = neg_us_early, work.tile([P, N], F32, name="neg_z")[:]
+            if j < LANES - 1:
+                neg_scale, neg_z = neg_us_in_lane[2 if j == 0 else 3], work.tile([P, N], F32, name="neg_z")[:]
             else:
                 neg_scale, neg_z = neg_us, head_diff[:, block(j, N)]
             return exponentials(j, banks[HEAD_LOGIT_BANKS[j]], head_scaled, neg_scale, neg_z, head_total[:, j : j + 1])
@@ -247,7 +254,7 @@ def tile_attend_gadsm_x_pl_kernel(tc, xT, wT, hT, us, ts, th, wt, wh, yt, yh, of
                 in_=bank[:].rearrange("p (n q) -> p q n", n=4),
             )
 
-        head_e = [head_exponentials(0), head_exponentials(1)]
+        head_e = [head_exponentials(j) for j in range(LANES - 1)]
         gather(2)
         gather(3)
         ts_columns = to_columns("ts_columns", banks[3], ts_listed)
@@ -261,10 +268,10 @@ def tile_attend_gadsm_x_pl_kernel(tc, xT, wT, hT, us, ts, th, wt, wh, yt, yh, of
         w_mx = []
         for n in range(LANES + 1):
             if n < LANES:
-                interleave(nc.vector.tensor_copy if n < LANES // 2 else nc.scalar.copy, w_rounded[:], w_lanes, n, LANES)
+                interleave(nc.vector.tensor_copy if n == 0 else nc.scalar.copy, w_rounded[:, block(n, N)], w_lanes[:, :, block(n)])
             if n > 0:
                 w_mx.append(quantized("w%d" % (n - 1), w_rounded[:, block(n - 1, N)], E4M3))
-        head_e.extend([head_exponentials(2), head_exponentials(3)])
+        head_e.append(head_exponentials(LANES - 1))
         tail_scaled = [
             scores("tail_scaled%d" % n, banks[TAIL_SCORE_BANKS[n]], w_mx[n], block(0), ts_columns[:, n : n + 1]) for n in range(LANES)
         ]
@@ -334,9 +341,9 @@ def tile_attend_gadsm_x_pl_kernel(tc, xT, wT, hT, us, ts, th, wt, wh, yt, yh, of
         out_rounded = kept("out_rounded", [P, LANES * N], BF16)
         out_mx = mx_tiles("out", N)
         result_lanes = result[:].rearrange("p (t c) -> p t c", t=LANES)
-        interleave(nc.vector.tensor_copy, out_rounded[:], result_lanes, 0, 2)
-        interleave(nc.vector.tensor_copy, out_rounded[:], result_lanes, 2, 4)
-        interleave(nc.scalar.copy, out_rounded[:], result_lanes, 3, 4)
+        interleave(nc.vector.tensor_copy, out_rounded[:, block(0, 2 * N)], result_lanes[:, :, block(0, N // 2)])
+        interleave(nc.vector.tensor_copy, out_rounded[:, block(2, N)], result_lanes[:, :, block(2)])
+        interleave(nc.scalar.copy, out_rounded[:, block(3, N)], result_lanes[:, :, block(3)])
         words_out = out_1.rearrange("o p c t -> p (o c t)").bitcast(I32)
         for half in range(2):
             columns = block(half, N // 2)

@@ -57,23 +57,21 @@ def tile_attend_gadsm_x_pl_kernel(tc, xT, wT, hT, us, ts, th, wt, wh, yt, yh, of
         nc.vector.memset(ts_window[:], 0.0)
         nc.scalar.dma_start(out=ts_window[0:1, :], in_=ts[0:1, :])
         th_lanes = kept("th_lanes", [P, LANES], F32)
-        nc.sync.dma_start(out=th_lanes[:], in_=th[0:1, :].rearrange("o (p t) -> p (o t)", t=LANES))
+        nc.scalar.dma_start(out=th_lanes[:], in_=th[0:1, :].rearrange("o (p t) -> p (o t)", t=LANES))
 
-        def load_halves(name, src):
+        def load_lanes(name, src):
             raw = kept(name, [P, LANES * N], F32)
-            halves = [raw[:, block(a, 2 * N)].rearrange("p (t c) -> p t c", t=LANES) for a in range(2)]
-            for a in range(2):
-                nc.sync.dma_start(out=halves[a], in_=src.rearrange("(p t) c -> p t c", t=LANES)[:, :, block(a, N // 2)])
-            return halves
+            nc.sync.dma_start(out=raw[:], in_=src.rearrange("(p t) c -> p (t c)", t=LANES))
+            return raw[:].rearrange("p (t c) -> p t c", t=LANES)
 
-        h_halves = load_halves("h_raw", hT)
-        x_halves = load_halves("x_raw", xT)
+        h_lanes = load_lanes("h_raw", hT)
+        x_lanes = load_lanes("x_raw", xT)
         offsets = kept("offsets", [P, N // 16], U16)
         nc.sync.dma_start(offsets[:], offs)
 
         def load_row_factors(name, src):
             factors = kept(name, [P, LANES], F32)
-            nc.sync.dma_start(out=factors[:], in_=src.rearrange("(q j) o -> q (j o)", j=LANES))
+            nc.scalar.dma_start(out=factors[:], in_=src.rearrange("(q j) o -> q (j o)", j=LANES))
             return factors
 
         us_rows = load_row_factors("us_rows", us)
@@ -135,10 +133,10 @@ def tile_attend_gadsm_x_pl_kernel(tc, xT, wT, hT, us, ts, th, wt, wh, yt, yh, of
             nc.scalar.copy(out=columns[:], in_=bank[:, 0:N:P])
             return columns
 
-        def along_d(name, halves, rounded):
+        def along_d(name, lanes, rounded):
             mx = mx_tiles(name, N)
             for a in range(2):
-                interleave(nc.vector.tensor_copy, rounded[:, block(a, 2 * N)], halves[a])
+                interleave(nc.vector.tensor_copy, rounded[:, block(a, 2 * N)], lanes[:, :, block(a, N // 2)])
             for a in range(2):
                 quantize(mx, block(a, N // 2), rounded[:, block(a, 2 * N)], E4M3)
             return mx
@@ -191,10 +189,10 @@ def tile_attend_gadsm_x_pl_kernel(tc, xT, wT, hT, us, ts, th, wt, wh, yt, yh, of
         th_columns = to_columns("th_columns", banks[1], th_rows)
 
         h_rounded = kept("h_rounded", [P, LANES * N], BF16)
-        h_mx = along_d("h", h_halves, h_rounded[:])
+        h_mx = along_d("h", h_lanes, h_rounded[:])
         PITCH = 3 * N
         shared = kept("shared", [P, LANES * PITCH], BF16)
-        x_mx = along_d("x", x_halves, shared[:, 0 : LANES * N])
+        x_mx = along_d("x", x_lanes, shared[:, 0 : LANES * N])
 
         h_turned = kept("h_turned", [P, LANES * N], BF16)
         h_pairs = h_rounded[:].bitcast(F32)
@@ -227,9 +225,9 @@ def tile_attend_gadsm_x_pl_kernel(tc, xT, wT, hT, us, ts, th, wt, wh, yt, yh, of
             scores("head_scaled%d" % n, banks[HEAD_SCORE_BANKS[n]], h_mx, block(n), th_columns[:, n : n + 1]) for n in range(LANES)
         ]
         h_rows_mx = quantized("h_rows", h_turned[:], E4M3)
+        gather(0)
         ts_listed = shared[:, N : 3 * N].bitcast(F32)
         nc.vector.tensor_copy(ts_listed, ts_window[:].indirect(offsets[:]))
-        gather(0)
         gather(1)
 
         head_diff = kept("head_diff", [P, TABLE], F32, tag="w_raw%d" % (LANES - 1))

from contextlib import ExitStack

import concourse.mybir as mybir
from concourse.masks import make_identity

F32 = mybir.dt.float32
BF16 = mybir.dt.bfloat16
U32 = mybir.dt.uint32
I32 = mybir.dt.int32
U16 = mybir.dt.uint16
U8 = mybir.dt.uint8
E4M3 = mybir.dt.float8_e4m3fn_x4
E5M2 = mybir.dt.float8_e5m2_x4
ALU = mybir.AluOpType
ACT = mybir.ActivationFunctionType

P = 128
LANES = 4
N = P * LANES
TABLE = 2048
BANKS = 8
FLOPS = 4 * 2 * N * N * N
BYTES = 4 * (5 * N * N + N * TABLE + TABLE + 4 * N) + 2 * P * N // 16 + N * N + 16 * N

HEAD_SCORE_BANKS = (0, 1, 2, 3)
HEAD_LOGIT_BANKS = (4, 5, 0, 1)
TAIL_SCORE_BANKS = (2, 3, 4, 5)
TAIL_LOGIT_BANKS = (0, 1, 2, 3)
HEAD_GRADIENT_BANKS = (6, 4, 5, 6)
TAIL_GRADIENT_BANKS = (6, 7, 6, 7)
RESULT_BANKS = (4, 5, 0, 1)
FINISH_LAG = 2


def block(n, width=P):
    return slice(n * width, (n + 1) * width)


def tile_attend_gadsm_x_pl_kernel(tc, xT, wT, hT, us, ts, th, wt, wh, yt, yh, offs, out_0, out_1, out_2):
    nc = tc.nc
    with ExitStack() as ctx:
        keep = ctx.enter_context(tc.tile_pool(name="keep", bufs=1))
        work = ctx.enter_context(tc.tile_pool(name="work", bufs=3))
        psum = ctx.enter_context(tc.psum_pool(name="psum", bufs=1))
        banks = [psum.tile([P, N], F32, name="bank%d" % n) for n in range(BANKS)]

        def kept(name, shape, dtype, tag=None):
            return keep.tile(shape, dtype, name=name, tag=tag or name, align_bytes=64)

        ident = kept("ident", [P, P], F32)
        make_identity(nc, ident[:])
        warm = kept("warm", [P, 1], F32)
        nc.vector.memset(warm[:], 0.0)
        nc.scalar.activation(warm[:], warm[:], ACT.Exp)

        ts_window = kept("ts_window", [P, TABLE], F32)
        nc.vector.memset(ts_window[:], 0.0)
        nc.scalar.dma_start(out=ts_window[0:1, :], in_=ts[0:1, :])
        th_lanes = kept("th_lanes", [P, LANES], F32)
        nc.scalar.dma_start(out=th_lanes[:], in_=th[0:1, :].rearrange("o (p t) -> p (o t)", t=LANES))

        def load_lanes(name, src):
            raw = kept(name, [P, LANES * N], F32)
            nc.sync.dma_start(out=raw[:], in_=src.rearrange("(p t) c -> p (t c)", t=LANES))
            return raw[:].rearrange("p (t c) -> p t c", t=LANES)

        h_lanes = load_lanes("h_raw", hT)
        x_lanes = load_lanes("x_raw", xT)
        offsets = kept("offsets", [P, N // 16], U16)
        nc.sync.dma_start(offsets[:], offs)

        def load_row_factors(name, src):
            factors = kept(name, [P, LANES], F32)
            nc.scalar.dma_start(out=factors[:], in_=src.rearrange("(q j) o -> q (j o)", j=LANES))
            return factors

        us_rows = load_row_factors("us_rows", us)
        wh_rows = load_row_factors("wh_rows", wh)
        wt_rows = load_row_factors("wt_rows", wt)
        w_raw = []
        for t in range(LANES):
            w_raw.append(kept("w_raw%d" % t, [P, TABLE], F32))
            nc.sync.dma_start(out=w_raw[t][:], in_=wT.rearrange("(p t) c -> t p c", t=LANES)[t])

        def load_targets(name, src):
            tiles = []
            for a in range(2):
                pair = kept(name + "%d" % a, [P, 2 * N], F32)
                nc.sync.dma_start(out=pair[:], in_=src.rearrange("(q a j) c -> a q (j c)", a=2, j=2)[a])
                tiles.extend([pair[:, block(0, N)], pair[:, block(1, N)]])
            return tiles

        yh_tiles = load_targets("yh", yh)
        yt_tiles = load_targets("yt", yt)

        def mx_tiles(name, columns):
            return kept(name + "_codes", [P, columns], U32), kept(name + "_scales", [P, columns], U8)

        def quantize(mx, columns, src, fmt):
            nc.vector.quantize_mx(out=mx[0][:, columns].bitcast(fmt), scales=mx[1][:, columns], in_=src)

        def quantized(name, src, fmt):
            columns = src.shape[1] // LANES
            mx = mx_tiles(name, columns)
            quantize(mx, slice(0, columns), src, fmt)
            return mx

        def multiply(bank, lhs, lhs_fmt, lhs_columns, rhs, start, stop):
            nc.tensor.matmul_mx(
                out=bank[:],
                lhsT=lhs[0][:, lhs_columns].bitcast(lhs_fmt),
                lhsT_scale=lhs[1][:, lhs_columns],
                rhs=rhs[0][:].bitcast(E4M3),
                rhs_scale=rhs[1][:],
                start=start,
                stop=stop,
            )

        def interleave(copy, dst, lanes):
            copy(
                out=dst.rearrange("p (c i t) -> p c t i", i=4, t=LANES),
                in_=lanes.rearrange("p t (c i) -> p c t i", i=4),
            )

        def spread(bank, columns):
            for n in range(LANES):
                nc.tensor.transpose(bank[:, block(n)], columns[:, n : n + 1].to_broadcast([P, P]), ident[:])

        def to_columns(name, bank, rows):
            for n in range(LANES):
                nc.tensor.transpose(bank[:, block(n)], rows[:, block(n)], ident[:])
            columns = kept(name, [P, LANES], F32)
            nc.scalar.copy(out=columns[:], in_=bank[:, 0:N:P])
            return columns

        def along_d(name, lanes, rounded):
            mx = mx_tiles(name, N)
            for a in range(2):
                interleave(nc.vector.tensor_copy, rounded[:, block(a, 2 * N)], lanes[:, :, block(a, N // 2)])
            for a in range(2):
                quantize(mx, block(a, N // 2), rounded[:, block(a, 2 * N)], E4M3)
            return mx

        def scores(name, bank, words, columns, scale):
            multiply(bank, words, E4M3, columns, x_mx, True, True)
            scaled = kept(name, [P, N], F32)
            nc.scalar.activation(
                scaled[:].rearrange("p (j q) -> p j q", j=LANES),
                bank[:].rearrange("p (q j) -> p j q", j=LANES),
                ACT.Copy,
                scale=scale,
            )
            return scaled

        def exponentials(j, bank, scaled, neg_scale, neg_z, total):
            for n in range(LANES):
                nc.tensor.transpose(bank[:, block(n)], scaled[n][:, block(j)], ident[:])
            neg_max = work.tile([P, 1], F32, name="neg_max", bufs=LANES)
            nc.vector.tensor_scalar(neg_z, bank[:], neg_scale[:, j : j + 1], None, ALU.mult, ALU.min, accum_out=neg_max[:])
            e = work.tile([P, N], F32, name="e", bufs=2 * LANES)
            nc.scalar.activation(e[:], neg_z, ACT.Exp, bias=neg_max[:], scale=-1.0, accum_out=total)
            return e

        def row_factors(name, total, neg_weight, a):
            inverse = kept(name + "_inverse%d" % a, [P, 2], F32)
            nc.vector.reciprocal(inverse[:], total[:, block(a, 2)])
            factor = kept(name + "_factor%d" % a, [P, 2], F32)
            nc.vector.tensor_tensor(factor[:], inverse[:], neg_weight[:, block(a, 2)], ALU.mult)
            return [factor[:, 0:1], factor[:, 1:2]]

        def gradient(bank, e, total, targets, factor, word_scales, diff, turned):
            nc.vector.scalar_tensor_tensor(diff, targets, total, e[:], ALU.mult, ALU.subtract)
            g = work.tile([P, N], BF16, name="g")
            nc.vector.scalar_tensor_tensor(g[:], diff, factor, word_scales[:], ALU.mult, ALU.mult)
            pairs = g[:].bitcast(F32)
            for v in range(2):
                nc.tensor.transpose(bank[:, block(v)], pairs[:, v : N // 2 : 2], ident[:])
            nc.scalar.copy(
                out=turned.bitcast(F32).rearrange("p (q v) -> p q v", v=2),
                in_=bank[:, 0 : 2 * P].rearrange("p (v q) -> p q v", v=2),
            )

        th_rows = kept("th_rows", [P, N], F32)
        spread(banks[0], th_lanes)
        nc.scalar.copy(
            out=th_rows[:].rearrange("m (p t) -> m p t", t=LANES),
            in_=banks[0][:].rearrange("m (t p) -> m p t", t=LANES),
        )
        th_columns = to_columns("th_columns", banks[1], th_rows)

        h_rounded = kept("h_rounded", [P, LANES * N], BF16)
        h_mx = along_d("h", h_lanes, h_rounded[:])
        PITCH = 3 * N
        shared = kept("shared", [P, LANES * PITCH], BF16)
        x_mx = along_d("x", x_lanes, shared[:, 0 : LANES * N])

        h_turned = kept("h_turned", [P, LANES * N], BF16)
        h_pairs = h_rounded[:].bitcast(F32)
        for v in range(2):
            bank = banks[2 + v]
            for t in range(LANES):
                nc.tensor.transpose(bank[:, block(t)], h_pairs[:, 2 * t + v : 2 * N : 2 * LANES], ident[:])
            nc.scalar.copy(
                out=h_turned[:].rearrange("q (p v s t) -> q v p s t", v=2, s=2, t=LANES)[:, v],
                in_=bank[:].bitcast(BF16).rearrange("q (t p s) -> q p s t", t=LANES, s=2),
            )

        neg_us = kept("neg_us", [P, LANES], F32)
        nc.gpsimd.tensor_scalar(neg_us[:], us_rows[:], -1.0, 0.0, ALU.mult, ALU.add)
        neg_us_in_lane = {t: shared[:, t * PITCH : t * PITCH + 2 * LANES].bitcast(F32) for t in (2, 3)}
        for t in (3, 2):
            nc.gpsimd.tensor_scalar(neg_us_in_lane[t], us_rows[:], -1.0, 0.0, ALU.mult, ALU.add)
        neg_head_weight = kept("neg_head_weight", [P, LANES], F32)
        nc.gpsimd.tensor_tensor(neg_head_weight[:], wh_rows[:], neg_us[:], ALU.mult)
        neg_tail_weight = kept("neg_tail_weight", [P, LANES], F32)
        nc.gpsimd.tensor_tensor(neg_tail_weight[:], wt_rows[:], neg_us[:], ALU.mult)

        def gathered(t):
            return shared[:, t * PITCH : t * PITCH + N]

        def gather(t):
            nc.vector.tensor_copy(gathered(t), w_raw[t][:].indirect(offsets[:]))

        head_scaled = [
            scores("head_scaled%d" % n, banks[HEAD_SCORE_BANKS[n]], h_mx, block(n), th_columns[:, n : n + 1]) for n in range(LANES)
        ]
        h_rows_mx = quantized("h_rows", h_turned[:], E4M3)
        gather(0)
        ts_listed = shared[:, N : 3 * N].bitcast(F32)
        nc.vector.tensor_copy(ts_listed, ts_window[:].indirect(offsets[:]))
        gather(1)

        head_diff = kept("head_diff", [P, TABLE], F32, tag="w_raw%d" % (LANES - 1))
        head_total = kept("head_total", [P, LANES], F32)

        def head_exponentials(j):
            if j < LANES - 1:
                neg_scale, neg_z = neg_us_in_lane[2 if j == 0 else 3], work.tile([P, N], F32, name="neg_z")[:]
            else:
                neg_scale, neg_z = neg_us, head_diff[:, block(j, N)]
            return exponentials(j, banks[HEAD_LOGIT_BANKS[j]], head_scaled, neg_scale, neg_z, head_total[:, j : j + 1])

        w_turned = kept("w_turned", [P, LANES * N], BF16)

        def turn_gathered(bank, a):
            for s in (1, 0):
                pairs = gathered(2 * a + s).bitcast(F32)
                for v in range(2):
                    nc.tensor.transpose(bank[:, block(2 * s + v)], pairs[:, v : N // 2 : 2], ident[:])
            nc.scalar.copy(
                out=w_turned[:].bitcast(F32).rearrange("p (q a n) -> p a q n", a=2, n=4)[:, a],
                in_=bank[:].rearrange("p (n q) -> p q n", n=4),
            )

        head_e = [head_exponentials(j) for j in range(LANES - 1)]
        gather(2)
        gather(3)
        ts_columns = to_columns("ts_columns", banks[3], ts_listed)
        turn_gathered(banks[4], 0)
        ts_rows = kept("ts_rows", [P, N], F32)
        spread(banks[5], ts_columns)
        nc.scalar.copy(out=ts_rows[:], in_=banks[5][:])

        w_rounded = kept("w_rounded", [P, LANES * N], BF16)
        w_lanes = shared[:].rearrange("p (t c) -> p t c", t=LANES)[:, :, 0:N]
        w_mx = []
        for n in range(LANES + 1):
            if n < LANES:
                interleave(nc.vector.tensor_copy if n == 0 else nc.scalar.copy, w_rounded[:, block(n, N)], w_lanes[:, :, block(n)])
            if n > 0:
                w_mx.append(quantized("w%d" % (n - 1), w_rounded[:, block(n - 1, N)], E4M3))
        head_e.append(head_exponentials(LANES - 1))
        tail_scaled = [
            scores("tail_scaled%d" % n, banks[TAIL_SCORE_BANKS[n]], w_mx[n], block(0), ts_columns[:, n : n + 1]) for n in range(LANES)
        ]
        turn_gathered(banks[7], 1)

        head_factor = []
        gh_turned = kept("gh_turned", [P, LANES * N], BF16)
        for j in range(LANES):
            if j % 2 == 0:
                head_factor.extend(row_factors("head", head_total, neg_head_weight, j // 2))
            gradient(
                banks[HEAD_GRADIENT_BANKS[j]],
                head_e[j],
                head_total[:, j : j + 1],
                yh_tiles[j],
                head_factor[j],
                th_rows,
                head_diff[:, block(j, N)],
                gh_turned[:, block(j, N)],
            )
        gh_mx = quantized("gh", gh_turned[:], E5M2)
        w_rows_mx = quantized("w_rows", w_turned[:], E4M3)

        tail_total = kept("tail_total", [P, LANES], F32)
        tail_e = []
        for j in range(LANES):
            neg_z = work.tile([P, N], F32, name="neg_z")
            tail_e.append(exponentials(j, banks[TAIL_LOGIT_BANKS[j]], tail_scaled, neg_us, neg_z[:], tail_total[:, j : j + 1]))

        result = kept("result", [P, LANES * N], F32)
        out_tiles = out_0.rearrange("(q j) d -> j q d", j=LANES)
        g_turned = [kept("g_turned%d" % j, [P, N], BF16) for j in range(LANES)]
        tail_factor = []

        def tail_gradient(j):
            if j % 2 == 0:
                tail_factor.extend(row_factors("tail", tail_total, neg_tail_weight, j // 2))
            diff = work.tile([P, N], F32, name="diff", bufs=2)
            gradient(
                banks[TAIL_GRADIENT_BANKS[j]],
                tail_e[j],
                tail_total[:, j : j + 1],
                yt_tiles[j],
                tail_factor[j],
                ts_rows,
                diff[:],
                g_turned[j][:],
            )

        def finish(j):
            g_mx = quantized("g%d" % j, g_turned[j][:], E5M2)
            bank = banks[RESULT_BANKS[j]]
            multiply(bank, gh_mx, E5M2, block(j), h_rows_mx, True, False)
            multiply(bank, g_mx, E5M2, block(0), w_rows_mx, False, True)
            parts = 2 if j == LANES - 1 else 1
            for part in range(parts):
                columns = block(part, N // parts)
                nc.scalar.copy(out=result[:, block(j, N)][:, columns], in_=bank[:, columns])
            nc.sync.dma_start(out=out_tiles[j], in_=result[:, block(j, N)])

        for j in range(LANES + FINISH_LAG):
            if j < LANES:
                tail_gradient(j)
            if j >= FINISH_LAG:
                finish(j - FINISH_LAG)

        out_rounded = kept("out_rounded", [P, LANES * N], BF16)
        out_mx = mx_tiles("out", N)
        result_lanes = result[:].rearrange("p (t c) -> p t c", t=LANES)
        interleave(nc.vector.tensor_copy, out_rounded[:, block(0, 2 * N)], result_lanes[:, :, block(0, N // 2)])
        interleave(nc.vector.tensor_copy, out_rounded[:, block(2, N)], result_lanes[:, :, block(2)])
        interleave(nc.scalar.copy, out_rounded[:, block(3, N)], result_lanes[:, :, block(3)])
        words_out = out_1.rearrange("o p c t -> p (o c t)").bitcast(I32)
        for half in range(2):
            columns = block(half, N // 2)
            quantize(out_mx, columns, out_rounded[:, block(half, 2 * N)], E4M3)
            nc.sync.dma_start(out=words_out[:, columns], in_=out_mx[0][:, columns].bitcast(I32))
        scales_out = out_2.rearrange("o b c -> (o b) c").bitcast(I32)
        for n in range(4):
            queue = nc.scalar if n % 2 else nc.sync
            queue.dma_start(out=scales_out[block(n, 4), :], in_=out_mx[1][32 * n : 32 * n + 4, :].bitcast(I32))
